import numpy as np
import ml_dtypes


def mxq(x, axis, fmt="e4m3"):
    dtype, down = {"e4m3": (ml_dtypes.float8_e4m3fn, 7), "e5m2": (ml_dtypes.float8_e5m2, 14)}[fmt]
    v = np.moveaxis(np.asarray(x, np.float32).astype(ml_dtypes.bfloat16).astype(np.float64), axis, -1)
    blocks = v.reshape(v.shape[:-1] + (-1, 32))
    amax = np.abs(blocks).max(-1, keepdims=True)
    byte = np.maximum(np.where(amax > 0, np.frexp(amax)[1] - 1 + 127, 0) - down, 1)
    scale = np.exp2(byte - 127.0)
    codes = (blocks / scale).astype(np.float32).astype(dtype).astype(np.float64)
    return np.moveaxis((codes * scale).reshape(v.shape), -1, axis)


WIDE = False


def mx_kscale(k):
    if not WIDE:
        return np.ones(k)
    levels = np.array([10, -10, 5, -5, 0])
    if k % 512:
        return np.exp2(np.random.permutation(np.resize(levels, k // 32))).repeat(32)
    a = np.empty((k // 512, 16))
    for p in range(k // 512):
        a[p, :8] = np.random.permutation(np.resize(levels, 8))
        for g in range(8):
            far = levels[np.abs(levels - a[p, g]) >= 10]
            a[p, g + 8] = far[np.random.randint(len(far))]
    return np.exp2(a.ravel()).repeat(32)


def f64(x):
    return np.asarray(x).astype(np.float64)


def striped(idx):
    return np.tile(np.asarray(idx).reshape(-1, 16).T, (8, 1)).astype(np.uint16)


def unstriped(offs):
    return offs[:16].T.reshape(-1).astype(np.int64)


E2M1 = np.array([0.0, 0.5, 1.0, 1.5, 2.0, 3.0, 4.0, 6.0, -0.0, -0.5, -1.0, -1.5, -2.0, -3.0, -4.0, -6.0])


def pack_weight(w, fmt):
    k, n = w.shape
    w = f64(np.asarray(w, np.float32).astype(ml_dtypes.bfloat16)).reshape(k // 32, 32, n)
    amax = np.abs(w).max(1)
    if fmt == "e4m3":
        byte = np.frexp(amax)[1] - 1 + 127 - 7
    else:
        mant, ex = np.frexp(amax / 6.0)
        byte = np.where(mant > 0.5, ex, ex - 1) + 127
    byte = np.clip(np.where(amax > 0, byte, 1), 1, 254)
    scaled = (w * np.exp2(127.0 - byte)[:, None, :]).reshape(k, n).astype(np.float32)
    by_word = np.ascontiguousarray(scaled.reshape(k // 512, 128, 4, n).transpose(0, 1, 3, 2))
    if fmt == "e4m3":
        words = by_word.astype(ml_dtypes.float8_e4m3fn).view(np.uint8)
    else:
        c = by_word.astype(ml_dtypes.float4_e2m1fn).view(np.uint8) & 0xF
        words = (c[..., 0::2] | (c[..., 1::2] << 4)).reshape(k // 512, 128, 2 * n)
    return np.ascontiguousarray(words), np.ascontiguousarray(byte.astype(np.uint8).reshape(k // 512, 16, n))


def unpack_weight(words, scales, fmt):
    g, _, n = scales.shape
    words = np.ascontiguousarray(words).reshape(g, 128, n, -1)
    if fmt == "e4m3":
        vals = words.view(ml_dtypes.float8_e4m3fn).astype(np.float64)
    else:
        nib = np.empty((g, 128, n, 4), np.uint8)
        nib[..., 0::2] = words & 0xF
        nib[..., 1::2] = words >> 4
        vals = E2M1[nib]
    vals = vals * np.repeat(np.exp2(scales.astype(np.float64) - 127.0), 8, axis=1)[..., None]
    return vals.transpose(0, 1, 3, 2).reshape(g * 512, n)


def bf(x):
    return np.asarray(x, np.float32).astype(ml_dtypes.bfloat16)


def planes(Y):
    r, m = Y.shape
    b = f64(bf(Y)).reshape(r // 32, 32, m)
    amax = np.abs(b).max(1)
    byte = np.clip(np.where(amax > 0, np.frexp(amax)[1] - 1 + 127 - 7, 1), 1, 254)
    codes = (b * np.exp2(127.0 - byte)[:, None, :]).reshape(r, m).astype(np.float32).astype(ml_dtypes.float8_e4m3fn).view(np.uint8)
    words = codes.reshape(r // 512, 128, 4, m).transpose(0, 1, 3, 2)
    return np.ascontiguousarray(words), np.ascontiguousarray(byte.astype(np.uint8).reshape(r // 512, 16, m))


D, T, I, Q, E, V = 512, 2048, 512, 256, 512, 32


def setup_inputs():
    n = np.random.standard_normal
    idx = np.random.permutation(T)[:I]
    idx4 = np.random.permutation(I)[:I]
    fd = mx_kscale(D)
    fi = mx_kscale(I)
    ti = np.ones(T)
    ti[idx] = fi
    keysp = pack_weight(n((D, T)) / fd[:, None], "e2m1")
    return {
        "query": (n((D, Q)) * 0.8 / np.sqrt(D) * fd[:, None]).astype(np.float32),
        "keys_words": keysp[0],
        "keys_scales": keysp[1],
        "lam": (np.random.uniform(0.05, 0.12, (1, Q))).astype(np.float32),
        "pull": (np.random.uniform(0.4, 1.2, (Q, 1))).astype(np.float32),
        "os": (np.random.uniform(4.0, 16.0, (1, I)) * fi).astype(np.float32),
        "vals": (n((E, T)) / ti).astype(np.float32),
        "memq": (np.random.uniform(0.3, 1.0, (1, Q))).astype(np.float32),
        "offs": striped(idx),
        "offs4": striped(idx4),
    }


def reference(query, keys_words, keys_scales, lam, pull, os, vals, memq, offs, offs4):
    idx = unstriped(offs)
    idx4 = unstriped(offs4)
    keysu = unpack_weight(keys_words, keys_scales, "e2m1")
    keysidxg = keysu[:, idx]
    queryq = mxq(f64(query), 0, "e4m3")
    a0 = keysidxg.T @ queryq
    ag = a0.reshape(I, V, Q // V).sum(axis=2)
    ar = np.repeat(ag, Q // V, axis=1)
    s0 = a0 - ar * f64(lam)
    s = s0.T
    p = np.exp(s - np.max(s, axis=1, keepdims=True))
    r = p / np.sum(p, axis=1, keepdims=True)
    w = r + r[:, idx4] * f64(pull)
    wo1 = w * f64(os)
    wt1 = wo1.T
    vt1 = f64(vals)[:, idx].T
    vt1q = mxq(vt1, 0, "e4m3")
    wt1q = mxq(wt1, 0, "e4m3")
    o = vt1q.T @ wt1q
    o1 = np.pad(o, ((0, 0), (1, 0)))[:, :Q]
    y = o - o1 * f64(memq)
    words, scales = planes(y)
    return y, words, scales

@@ -1,0 +1,268 @@
+from contextlib import ExitStack
+
+import concourse.mybir as mybir
+from concourse.masks import make_identity
+
+D, T, I, Q, E = 512, 2048, 512, 256, 512
+FLOPS = 2 * D * I * Q + 2 * I * E * Q
+
+F32 = mybir.dt.float32
+BF16 = mybir.dt.bfloat16
+I32 = mybir.dt.int32
+U32 = mybir.dt.uint32
+U16 = mybir.dt.uint16
+U8 = mybir.dt.uint8
+FP8X4 = mybir.dt.float8_e4m3fn_x4
+FP4X4 = mybir.dt.float4_e2m1fn_x4
+ALU = mybir.AluOpType
+ACT = mybir.ActivationFunctionType
+AXIS = mybir.AxisListType
+
+P = 128
+PACK = 4
+GROUP = 8
+HALVES = Q // P
+
+
+def tile_attend_beyondgroup_followed_rowchanges_pl_kernel(
+    tc, query, keys_words, keys_scales, lam, pull, slot_factor, vals, memq, offs, offs4, out_0, out_1, out_2
+):
+    nc = tc.nc
+    with ExitStack() as ctx:
+        sb = ctx.enter_context(tc.tile_pool(name="sb", bufs=1))
+        ps = ctx.enter_context(tc.psum_pool(name="ps", bufs=1))
+
+        def quantize(grouped, codes, scales):
+            nc.vector.quantize_mx(out=codes.bitcast(FP8X4), scales=scales, in_=grouped)
+
+        slots = sb.tile([P, I // 16], U16, name="slots")
+        nc.sync.dma_start(slots[:], offs)
+        followed = sb.tile([P, I // 16], U16, name="followed")
+        nc.sync.dma_start(followed[:], offs4)
+        lam_rows = sb.tile([P, P], F32, name="lam_rows")
+        nc.gpsimd.memset(lam_rows[:], 0.0)
+        nc.scalar.dma_start(lam_rows[0:2, :], lam.rearrange("o (c n) -> (o c) n", n=P))
+        key_scale_pool = sb.tile([P, T], U8, name="key_scale_pool", tag="pool1", align_bytes=64)
+        nc.vector.memset(key_scale_pool[:].bitcast(I32), 0)
+        for quad in range(4):
+            nc.scalar.dma_start(
+                key_scale_pool[32 * quad : 32 * quad + 4, :].bitcast(I32),
+                keys_scales[0, 4 * quad : 4 * quad + 4, :].bitcast(I32),
+            )
+        key_word_pool = sb.tile([P, T], U16, name="key_word_pool", tag="pool2", align_bytes=64)
+        nc.sync.dma_start(key_word_pool[:].bitcast(I32), keys_words[0].bitcast(I32))
+        query_raw = sb.tile([P, PACK, Q], F32, name="query_raw", tag="pool3", align_bytes=64)
+        nc.sync.dma_start(query_raw[:], query.rearrange("(p t) q -> p t q", t=PACK))
+
+        ident = sb.tile([P, P], F32, name="ident")
+        make_identity(nc, ident[:])
+        factor_rows = sb.tile([P, P], F32, name="factor_rows")
+        nc.gpsimd.memset(factor_rows[:], 0.0)
+        nc.gpsimd.dma_start(factor_rows[0:4, :], slot_factor.rearrange("o (c n) -> (o c) n", n=P))
+        nc.gpsimd.dma_start(factor_rows[4:6, :], pull.rearrange("(c n) o -> c (n o)", n=P))
+        nc.gpsimd.dma_start(factor_rows[6:8, :], memq.rearrange("o (c n) -> (o c) n", n=P))
+
+        vals_rows = vals.rearrange("(p t) c -> t p c", t=PACK)
+        val_pool = []
+
+        def load_values(t):
+            pool = sb.tile([P, T], F32, name=f"val_pool{t}", tag=f"pool{t}", align_bytes=64)
+            nc.sync.dma_start(pool[:], vals_rows[t])
+            val_pool.append(pool)
+
+        load_values(0)
+
+        key_scales = sb.tile([P, I], U8, name="key_scales", align_bytes=64)
+        nc.vector.tensor_copy(key_scales[:], key_scale_pool[:].indirect(slots[:]))
+        key_words = sb.tile([P, I], U16, name="key_words", align_bytes=64)
+        nc.vector.tensor_copy(key_words[:], key_word_pool[:].indirect(slots[:]))
+
+        query_codes, query_scales = [], []
+        for h in range(HALVES):
+            grouped = sb.tile([P, P * PACK], BF16, name=f"query_grouped{h}", align_bytes=64)
+            nc.scalar.copy(
+                grouped[:].rearrange("p (c i t) -> p c t i", i=4, t=PACK),
+                query_raw[:, :, h * P : (h + 1) * P].rearrange("p t (c i) -> p c t i", i=4),
+            )
+            codes = sb.tile([P, P], U32, name=f"query_codes{h}", align_bytes=64)
+            scales = sb.tile([P, P], U8, name=f"query_scales{h}", align_bytes=64)
+            quantize(grouped[:], codes[:], scales[:])
+            query_codes.append(codes)
+            query_scales.append(scales)
+
+        for t in range(1, PACK):
+            load_values(t)
+
+        lam_turned = ps.tile([P, P], F32, name="lam_turned", tag="values0")
+        nc.tensor.transpose(lam_turned[:], lam_rows[:], ident[:])
+        lam_cols = sb.tile([P, 2], F32, name="lam_cols")
+        nc.vector.tensor_scalar(lam_cols[:], lam_turned[:, 0:2], -1.0, None, ALU.mult)
+        neg_lam_row = ps.tile([P, Q], F32, name="neg_lam_row", tag="spread")
+        for c in range(2):
+            nc.tensor.transpose(neg_lam_row[:, c * P : (c + 1) * P], lam_cols[:, c : c + 1].to_broadcast([P, P]), ident[:])
+        factor_cols = sb.tile([P, 8], F32, name="factor_cols")
+        os_row = ps.tile([P, I], F32, name="os_row", tag="os_row")
+        memq_row = sb.tile([P, Q], F32, name="memq_row")
+
+        def spread_factors():
+            turned_rows = ps.tile([P, P], F32, name="turned_rows", tag="values1")
+            nc.tensor.transpose(turned_rows[:], factor_rows[:], ident[:])
+            nc.scalar.copy(factor_cols[:], turned_rows[:, 0:8])
+            for c in range(4):
+                nc.tensor.transpose(os_row[:, c * P : (c + 1) * P], factor_cols[:, c : c + 1].to_broadcast([P, P]), ident[:])
+            memq_spread = ps.tile([P, Q], F32, name="memq_spread", tag="values0")
+            for c in range(2):
+                nc.tensor.transpose(memq_spread[:, c * P : (c + 1) * P], factor_cols[:, 6 + c : 7 + c].to_broadcast([P, P]), ident[:])
+            nc.scalar.copy(memq_row[:], memq_spread[:])
+
+        lagged = sb.tile([P, PACK, Q], F32, name="lagged")
+        nc.vector.memset(lagged[:, :, 0:1], 0.0)
+
+        def turn_pairs(rounded, bank_tag, name):
+            words = rounded[:].bitcast(F32)
+            turned = ps.tile([P, 2, P], F32, name=f"{name}_turned", tag=bank_tag)
+            for u in range(2):
+                nc.tensor.transpose(turned[:, u, :], words[:, u : 2 * P : 2], ident[:])
+            grouped = sb.tile([P, P * PACK], BF16, name=f"{name}_grouped", align_bytes=64)
+            nc.scalar.copy(
+                grouped[:].bitcast(F32).rearrange("p (x u) -> p x u", u=2),
+                turned[:].rearrange("p u x -> p x u"),
+            )
+            codes = sb.tile([P, P], U32, name=f"{name}_codes", align_bytes=64)
+            scales = sb.tile([P, P], U8, name=f"{name}_scales", align_bytes=64)
+            quantize(grouped[:], codes[:], scales[:])
+            return codes, scales
+
+        def products(h):
+            a0 = ps.tile([P, 4, P], F32, name=f"a0_{h}", tag=f"product{h}")
+            for it in range(4):
+                cols = slice(it * P, (it + 1) * P)
+                nc.tensor.matmul_mx(
+                    out=a0[:, it, :],
+                    lhsT=key_words[:, cols].bitcast(FP4X4),
+                    lhsT_scale=key_scales[:, cols],
+                    rhs=query_codes[h][:].bitcast(FP8X4),
+                    rhs_scale=query_scales[h][:],
+                    start=True,
+                    stop=True,
+                )
+            ag = sb.tile([P, 4 * P // GROUP], F32, name=f"ag{h}")
+            nc.vector.tensor_reduce(
+                ag[:], a0[:].rearrange("p a (v j) -> p (a v) j", j=GROUP), axis=AXIS.X, op=ALU.add
+            )
+            a0_sb = sb.tile([P, 4, P], F32, name=f"a0_sb{h}")
+            nc.scalar.copy(a0_sb[:], a0[:])
+            return ag, a0_sb
+
+        def scores(h, ag, a0_sb):
+            shape = [P, 4, P // GROUP, GROUP]
+            cut = sb.tile([P, 4, P], F32, name=f"cut{h}")
+            nc.vector.tensor_tensor(
+                cut[:].rearrange("p a (v j) -> p a v j", j=GROUP),
+                ag[:].rearrange("p (a v) -> p a v", a=4).unsqueeze(3).to_broadcast(shape),
+                neg_lam_row[:, h * P : (h + 1) * P].rearrange("p (v j) -> p v j", j=GROUP).unsqueeze(1).to_broadcast(shape),
+                ALU.mult,
+            )
+            s = ps.tile([P, I], F32, name=f"s{h}", tag=f"turn{h}")
+            terms = [(src, it) for src in (a0_sb, cut) for it in range(4)]
+            for n, (src, it) in enumerate(terms):
+                nc.tensor.matmul(
+                    s[:, it * P : (it + 1) * P],
+                    lhsT=src[:, it, :],
+                    rhs=ident[:],
+                    is_transpose=True,
+                    start=(n == 0),
+                    stop=(n == len(terms) - 1),
+                )
+            return s
+
+        def exponentials(h, s):
+            neg_max = sb.tile([P, 1], F32, name=f"neg_max{h}")
+            nc.vector.tensor_reduce(neg_max[:], s[:], axis=AXIS.X, op=ALU.max, negate=True)
+            p = sb.tile([P, I], F32, name=f"p{h}")
+            total = sb.tile([P, 1], F32, name=f"total{h}")
+            nc.scalar.activation(p[:], s[:], ACT.Exp, bias=neg_max[:], scale=1.0, accum_out=total[:])
+            return p, total
+
+        def shares(h, p, total):
+            inv = sb.tile([P, 1], F32, name=f"inv{h}")
+            nc.vector.reciprocal(inv[:], total[:])
+            r = sb.tile([P, I], F32, name=f"r{h}")
+            nc.vector.tensor_scalar(r[:], p[:], inv[:], None, ALU.mult)
+            looked = sb.tile([P, I], F32, name=f"looked{h}")
+            nc.vector.tensor_copy(looked[:, 0:256], r[:].indirect(followed[:, 0:16]))
+            nc.scalar.activation(looked[:, 256:512], r[:].indirect(followed[:, 16:32]), ACT.Copy)
+            return r, looked
+
+        def weights(h, r, looked):
+            w = sb.tile([P, I], F32, name=f"w{h}")
+            nc.vector.scalar_tensor_tensor(w[:], looked[:], factor_cols[:, 4 + h : 5 + h], r[:], ALU.mult, ALU.add)
+            wo = sb.tile([P, I], BF16, name=f"wo{h}")
+            nc.vector.tensor_tensor(wo[:], w[:], os_row[:], ALU.mult)
+            return turn_pairs(wo, f"turn{h}", f"w{h}")
+
+        def values(t):
+            picked = sb.tile([P, I], BF16, name=f"picked{t}")
+            if t == PACK - 1:
+                nc.vector.tensor_copy(picked[:], val_pool[t][:].indirect(slots[:]))
+            else:
+                nc.scalar.activation(picked[:], val_pool[t][:].indirect(slots[:]), ACT.Copy)
+            return turn_pairs(picked, f"values{t % 2}", f"v{t}")
+
+        y_scales = sb.tile([P, Q], U8, name="y_scales", align_bytes=64)
+        out_rows = out_0.rearrange("(p t) q -> p t q", t=PACK)
+        out_words = out_1[0].rearrange("p c r -> p (c r)").bitcast(I32)
+
+        def result(h, w_mx, v_mx):
+            o = ps.tile([P, PACK, P], F32, name=f"o{h}", tag=f"product{h}")
+            for t in range(PACK):
+                nc.tensor.matmul_mx(
+                    out=o[:, t, :],
+                    lhsT=v_mx[t][0][:].bitcast(FP8X4),
+                    lhsT_scale=v_mx[t][1][:],
+                    rhs=w_mx[0][:].bitcast(FP8X4),
+                    rhs_scale=w_mx[1][:],
+                    start=True,
+                    stop=True,
+                )
+            first = h * P + 1
+            count = min(P, Q - first)
+            nc.vector.tensor_tensor(
+                lagged[:, :, first : first + count],
+                o[:, :, 0:count],
+                memq_row[:, first : first + count].unsqueeze(1).to_broadcast([P, PACK, count]),
+                ALU.mult,
+            )
+            y = sb.tile([P, PACK, P], F32, name=f"y{h}")
+            nc.vector.tensor_tensor(y[:], o[:], lagged[:, :, h * P : (h + 1) * P], ALU.subtract)
+            nc.sync.dma_start(out_rows[:, :, h * P : (h + 1) * P], y[:])
+            grouped = sb.tile([P, P * PACK], BF16, name=f"y_grouped{h}", align_bytes=64)
+            cast = nc.scalar.copy if h == 0 else nc.vector.tensor_copy
+            cast(
+                grouped[:].rearrange("p (c i t) -> p c t i", i=4, t=PACK),
+                y[:].rearrange("p t (c i) -> p c t i", i=4),
+            )
+            codes = sb.tile([P, P], U32, name=f"y_codes{h}", align_bytes=64)
+            quantize(grouped[:], codes[:], y_scales[:, h * P : (h + 1) * P])
+            nc.sync.dma_start(out_words[:, h * P : (h + 1) * P], codes[:].bitcast(I32))
+
+        halves = range(HALVES)
+        sums = [products(h) for h in halves]
+        s_banks = [scores(h, *sums[h]) for h in halves]
+        spread_factors()
+        exps = [exponentials(h, s_banks[h]) for h in halves]
+        v_mx = [values(0)]
+        looks = [shares(h, *exps[h]) for h in halves]
+        w_mx = [weights(0, *looks[0])]
+        v_mx.append(values(1))
+        w_mx.append(weights(1, *looks[1]))
+        v_mx.append(values(2))
+        v_mx.append(values(3))
+        for h in range(HALVES):
+            result(h, w_mx[h], v_mx)
+        for quad in range(4):
+            queue = nc.scalar if quad % 2 else nc.sync
+            queue.dma_start(
+                out_2[0, 4 * quad : 4 * quad + 4, :].bitcast(I32),
+                y_scales[32 * quad : 32 * quad + 4, :].bitcast(I32),
+            )

@@ -37,15 +37,11 @@ def tile_attend_beyondgroup_followed_rowchanges_pl_kernel(
 
         slots = sb.tile([P, I // 16], U16, name="slots")
         nc.sync.dma_start(slots[:], offs)
-        followed = sb.tile([P, I // 16], U16, name="followed")
-        nc.sync.dma_start(followed[:], offs4)
-        lam_rows = sb.tile([P, P], F32, name="lam_rows")
-        nc.gpsimd.memset(lam_rows[:], 0.0)
-        nc.scalar.dma_start(lam_rows[0:2, :], lam.rearrange("o (c n) -> (o c) n", n=P))
         key_scale_pool = sb.tile([P, T], U8, name="key_scale_pool", tag="pool1", align_bytes=64)
-        nc.vector.memset(key_scale_pool[:].bitcast(I32), 0)
+        nc.gpsimd.memset(key_scale_pool[:].bitcast(I32), 0)
         for quad in range(4):
-            nc.scalar.dma_start(
+            queue = nc.scalar if quad < 2 else nc.sync
+            queue.dma_start(
                 key_scale_pool[32 * quad : 32 * quad + 4, :].bitcast(I32),
                 keys_scales[0, 4 * quad : 4 * quad + 4, :].bitcast(I32),
             )
@@ -53,9 +49,14 @@ def tile_attend_beyondgroup_followed_rowchanges_pl_kernel(
         nc.sync.dma_start(key_word_pool[:].bitcast(I32), keys_words[0].bitcast(I32))
         query_raw = sb.tile([P, PACK, Q], F32, name="query_raw", tag="pool3", align_bytes=64)
         nc.sync.dma_start(query_raw[:], query.rearrange("(p t) q -> p t q", t=PACK))
+        followed = sb.tile([P, I // 16], U16, name="followed")
+        nc.sync.dma_start(followed[:], offs4)
 
         ident = sb.tile([P, P], F32, name="ident")
         make_identity(nc, ident[:])
+        lam_rows = sb.tile([P, P], F32, name="lam_rows")
+        nc.vector.memset(lam_rows[:], 0.0)
+        nc.scalar.dma_start(lam_rows[0:2, :], lam.rearrange("o (c n) -> (o c) n", n=P))
         factor_rows = sb.tile([P, P], F32, name="factor_rows")
         nc.gpsimd.memset(factor_rows[:], 0.0)
         nc.gpsimd.dma_start(factor_rows[0:4, :], slot_factor.rearrange("o (c n) -> (o c) n", n=P))
@@ -203,10 +204,7 @@ def tile_attend_beyondgroup_followed_rowchanges_pl_kernel(
 
         def values(t):
             picked = sb.tile([P, I], BF16, name=f"picked{t}")
-            if t == PACK - 1:
-                nc.vector.tensor_copy(picked[:], val_pool[t][:].indirect(slots[:]))
-            else:
-                nc.scalar.activation(picked[:], val_pool[t][:].indirect(slots[:]), ACT.Copy)
+            nc.scalar.activation(picked[:], val_pool[t][:].indirect(slots[:]), ACT.Copy)
             return turn_pairs(picked, f"values{t % 2}", f"v{t}")
 
         y_scales = sb.tile([P, Q], U8, name="y_scales", align_bytes=64)

from contextlib import ExitStack

import concourse.mybir as mybir
from concourse.masks import make_identity

D, T, I, Q, E = 512, 2048, 512, 256, 512
FLOPS = 2 * D * I * Q + 2 * I * E * Q

F32 = mybir.dt.float32
BF16 = mybir.dt.bfloat16
I32 = mybir.dt.int32
U32 = mybir.dt.uint32
U16 = mybir.dt.uint16
U8 = mybir.dt.uint8
FP8X4 = mybir.dt.float8_e4m3fn_x4
FP4X4 = mybir.dt.float4_e2m1fn_x4
ALU = mybir.AluOpType
ACT = mybir.ActivationFunctionType
AXIS = mybir.AxisListType

P = 128
PACK = 4
GROUP = 8
HALVES = Q // P


def tile_attend_beyondgroup_followed_rowchanges_pl_kernel(
    tc, query, keys_words, keys_scales, lam, pull, slot_factor, vals, memq, offs, offs4, out_0, out_1, out_2
):
    nc = tc.nc
    with ExitStack() as ctx:
        sb = ctx.enter_context(tc.tile_pool(name="sb", bufs=1))
        ps = ctx.enter_context(tc.psum_pool(name="ps", bufs=1))

        def quantize(grouped, codes, scales):
            nc.vector.quantize_mx(out=codes.bitcast(FP8X4), scales=scales, in_=grouped)

        slots = sb.tile([P, I // 16], U16, name="slots")
        nc.sync.dma_start(slots[:], offs)
        key_scale_pool = sb.tile([P, T], U8, name="key_scale_pool", tag="pool1", align_bytes=64)
        nc.gpsimd.memset(key_scale_pool[:].bitcast(I32), 0)
        for quad in range(4):
            queue = nc.scalar if quad < 2 else nc.sync
            queue.dma_start(
                key_scale_pool[32 * quad : 32 * quad + 4, :].bitcast(I32),
                keys_scales[0, 4 * quad : 4 * quad + 4, :].bitcast(I32),
            )
        key_word_pool = sb.tile([P, T], U16, name="key_word_pool", tag="pool2", align_bytes=64)
        nc.sync.dma_start(key_word_pool[:].bitcast(I32), keys_words[0].bitcast(I32))
        query_raw = sb.tile([P, PACK, Q], F32, name="query_raw", tag="pool3", align_bytes=64)
        nc.sync.dma_start(query_raw[:], query.rearrange("(p t) q -> p t q", t=PACK))
        followed = sb.tile([P, I // 16], U16, name="followed")
        nc.sync.dma_start(followed[:], offs4)

        ident = sb.tile([P, P], F32, name="ident")
        make_identity(nc, ident[:])
        lam_rows = sb.tile([P, P], F32, name="lam_rows")
        nc.vector.memset(lam_rows[:], 0.0)
        nc.scalar.dma_start(lam_rows[0:2, :], lam.rearrange("o (c n) -> (o c) n", n=P))
        factor_rows = sb.tile([P, P], F32, name="factor_rows")
        nc.gpsimd.memset(factor_rows[:], 0.0)
        nc.gpsimd.dma_start(factor_rows[0:4, :], slot_factor.rearrange("o (c n) -> (o c) n", n=P))
        nc.gpsimd.dma_start(factor_rows[4:6, :], pull.rearrange("(c n) o -> c (n o)", n=P))
        nc.gpsimd.dma_start(factor_rows[6:8, :], memq.rearrange("o (c n) -> (o c) n", n=P))

        vals_rows = vals.rearrange("(p t) c -> t p c", t=PACK)
        val_pool = []

        def load_values(t):
            pool = sb.tile([P, T], F32, name=f"val_pool{t}", tag=f"pool{t}", align_bytes=64)
            nc.sync.dma_start(pool[:], vals_rows[t])
            val_pool.append(pool)

        load_values(0)

        key_scales = sb.tile([P, I], U8, name="key_scales", align_bytes=64)
        nc.vector.tensor_copy(key_scales[:], key_scale_pool[:].indirect(slots[:]))
        key_words = sb.tile([P, I], U16, name="key_words", align_bytes=64)
        nc.vector.tensor_copy(key_words[:], key_word_pool[:].indirect(slots[:]))

        query_codes, query_scales = [], []
        for h in range(HALVES):
            grouped = sb.tile([P, P * PACK], BF16, name=f"query_grouped{h}", align_bytes=64)
            nc.scalar.copy(
                grouped[:].rearrange("p (c i t) -> p c t i", i=4, t=PACK),
                query_raw[:, :, h * P : (h + 1) * P].rearrange("p t (c i) -> p c t i", i=4),
            )
            codes = sb.tile([P, P], U32, name=f"query_codes{h}", align_bytes=64)
            scales = sb.tile([P, P], U8, name=f"query_scales{h}", align_bytes=64)
            quantize(grouped[:], codes[:], scales[:])
            query_codes.append(codes)
            query_scales.append(scales)

        for t in range(1, PACK):
            load_values(t)

        lam_turned = ps.tile([P, P], F32, name="lam_turned", tag="values0")
        nc.tensor.transpose(lam_turned[:], lam_rows[:], ident[:])
        lam_cols = sb.tile([P, 2], F32, name="lam_cols")
        nc.vector.tensor_scalar(lam_cols[:], lam_turned[:, 0:2], -1.0, None, ALU.mult)
        neg_lam_row = ps.tile([P, Q], F32, name="neg_lam_row", tag="spread")
        for c in range(2):
            nc.tensor.transpose(neg_lam_row[:, c * P : (c + 1) * P], lam_cols[:, c : c + 1].to_broadcast([P, P]), ident[:])
        factor_cols = sb.tile([P, 8], F32, name="factor_cols")
        os_row = ps.tile([P, I], F32, name="os_row", tag="os_row")
        memq_row = sb.tile([P, Q], F32, name="memq_row")

        def spread_factors():
            turned_rows = ps.tile([P, P], F32, name="turned_rows", tag="values1")
            nc.tensor.transpose(turned_rows[:], factor_rows[:], ident[:])
            nc.scalar.copy(factor_cols[:], turned_rows[:, 0:8])
            for c in range(4):
                nc.tensor.transpose(os_row[:, c * P : (c + 1) * P], factor_cols[:, c : c + 1].to_broadcast([P, P]), ident[:])
            memq_spread = ps.tile([P, Q], F32, name="memq_spread", tag="values0")
            for c in range(2):
                nc.tensor.transpose(memq_spread[:, c * P : (c + 1) * P], factor_cols[:, 6 + c : 7 + c].to_broadcast([P, P]), ident[:])
            nc.scalar.copy(memq_row[:], memq_spread[:])

        lagged = sb.tile([P, PACK, Q], F32, name="lagged")
        nc.vector.memset(lagged[:, :, 0:1], 0.0)

        def turn_pairs(rounded, bank_tag, name):
            words = rounded[:].bitcast(F32)
            turned = ps.tile([P, 2, P], F32, name=f"{name}_turned", tag=bank_tag)
            for u in range(2):
                nc.tensor.transpose(turned[:, u, :], words[:, u : 2 * P : 2], ident[:])
            grouped = sb.tile([P, P * PACK], BF16, name=f"{name}_grouped", align_bytes=64)
            nc.scalar.copy(
                grouped[:].bitcast(F32).rearrange("p (x u) -> p x u", u=2),
                turned[:].rearrange("p u x -> p x u"),
            )
            codes = sb.tile([P, P], U32, name=f"{name}_codes", align_bytes=64)
            scales = sb.tile([P, P], U8, name=f"{name}_scales", align_bytes=64)
            quantize(grouped[:], codes[:], scales[:])
            return codes, scales

        def products(h):
            a0 = ps.tile([P, 4, P], F32, name=f"a0_{h}", tag=f"product{h}")
            for it in range(4):
                cols = slice(it * P, (it + 1) * P)
                nc.tensor.matmul_mx(
                    out=a0[:, it, :],
                    lhsT=key_words[:, cols].bitcast(FP4X4),
                    lhsT_scale=key_scales[:, cols],
                    rhs=query_codes[h][:].bitcast(FP8X4),
                    rhs_scale=query_scales[h][:],
                    start=True,
                    stop=True,
                )
            ag = sb.tile([P, 4 * P // GROUP], F32, name=f"ag{h}")
            nc.vector.tensor_reduce(
                ag[:], a0[:].rearrange("p a (v j) -> p (a v) j", j=GROUP), axis=AXIS.X, op=ALU.add
            )
            a0_sb = sb.tile([P, 4, P], F32, name=f"a0_sb{h}")
            nc.scalar.copy(a0_sb[:], a0[:])
            return ag, a0_sb

        def scores(h, ag, a0_sb):
            shape = [P, 4, P // GROUP, GROUP]
            cut = sb.tile([P, 4, P], F32, name=f"cut{h}")
            nc.vector.tensor_tensor(
                cut[:].rearrange("p a (v j) -> p a v j", j=GROUP),
                ag[:].rearrange("p (a v) -> p a v", a=4).unsqueeze(3).to_broadcast(shape),
                neg_lam_row[:, h * P : (h + 1) * P].rearrange("p (v j) -> p v j", j=GROUP).unsqueeze(1).to_broadcast(shape),
                ALU.mult,
            )
            s = ps.tile([P, I], F32, name=f"s{h}", tag=f"turn{h}")
            terms = [(src, it) for src in (a0_sb, cut) for it in range(4)]
            for n, (src, it) in enumerate(terms):
                nc.tensor.matmul(
                    s[:, it * P : (it + 1) * P],
                    lhsT=src[:, it, :],
                    rhs=ident[:],
                    is_transpose=True,
                    start=(n == 0),
                    stop=(n == len(terms) - 1),
                )
            return s

        def exponentials(h, s):
            neg_max = sb.tile([P, 1], F32, name=f"neg_max{h}")
            nc.vector.tensor_reduce(neg_max[:], s[:], axis=AXIS.X, op=ALU.max, negate=True)
            p = sb.tile([P, I], F32, name=f"p{h}")
            total = sb.tile([P, 1], F32, name=f"total{h}")
            nc.scalar.activation(p[:], s[:], ACT.Exp, bias=neg_max[:], scale=1.0, accum_out=total[:])
            return p, total

        def shares(h, p, total):
            inv = sb.tile([P, 1], F32, name=f"inv{h}")
            nc.vector.reciprocal(inv[:], total[:])
            r = sb.tile([P, I], F32, name=f"r{h}")
            nc.vector.tensor_scalar(r[:], p[:], inv[:], None, ALU.mult)
            looked = sb.tile([P, I], F32, name=f"looked{h}")
            nc.vector.tensor_copy(looked[:, 0:256], r[:].indirect(followed[:, 0:16]))
            nc.scalar.activation(looked[:, 256:512], r[:].indirect(followed[:, 16:32]), ACT.Copy)
            return r, looked

        def weights(h, r, looked):
            w = sb.tile([P, I], F32, name=f"w{h}")
            nc.vector.scalar_tensor_tensor(w[:], looked[:], factor_cols[:, 4 + h : 5 + h], r[:], ALU.mult, ALU.add)
            wo = sb.tile([P, I], BF16, name=f"wo{h}")
            nc.vector.tensor_tensor(wo[:], w[:], os_row[:], ALU.mult)
            return turn_pairs(wo, f"turn{h}", f"w{h}")

        def values(t):
            picked = sb.tile([P, I], BF16, name=f"picked{t}")
            nc.scalar.activation(picked[:], val_pool[t][:].indirect(slots[:]), ACT.Copy)
            return turn_pairs(picked, f"values{t % 2}", f"v{t}")

        y_scales = sb.tile([P, Q], U8, name="y_scales", align_bytes=64)
        out_rows = out_0.rearrange("(p t) q -> p t q", t=PACK)
        out_words = out_1[0].rearrange("p c r -> p (c r)").bitcast(I32)

        def result(h, w_mx, v_mx):
            o = ps.tile([P, PACK, P], F32, name=f"o{h}", tag=f"product{h}")
            for t in range(PACK):
                nc.tensor.matmul_mx(
                    out=o[:, t, :],
                    lhsT=v_mx[t][0][:].bitcast(FP8X4),
                    lhsT_scale=v_mx[t][1][:],
                    rhs=w_mx[0][:].bitcast(FP8X4),
                    rhs_scale=w_mx[1][:],
                    start=True,
                    stop=True,
                )
            first = h * P + 1
            count = min(P, Q - first)
            nc.vector.tensor_tensor(
                lagged[:, :, first : first + count],
                o[:, :, 0:count],
                memq_row[:, first : first + count].unsqueeze(1).to_broadcast([P, PACK, count]),
                ALU.mult,
            )
            y = sb.tile([P, PACK, P], F32, name=f"y{h}")
            nc.vector.tensor_tensor(y[:], o[:], lagged[:, :, h * P : (h + 1) * P], ALU.subtract)
            nc.sync.dma_start(out_rows[:, :, h * P : (h + 1) * P], y[:])
            grouped = sb.tile([P, P * PACK], BF16, name=f"y_grouped{h}", align_bytes=64)
            cast = nc.scalar.copy if h == 0 else nc.vector.tensor_copy
            cast(
                grouped[:].rearrange("p (c i t) -> p c t i", i=4, t=PACK),
                y[:].rearrange("p t (c i) -> p c t i", i=4),
            )
            codes = sb.tile([P, P], U32, name=f"y_codes{h}", align_bytes=64)
            quantize(grouped[:], codes[:], y_scales[:, h * P : (h + 1) * P])
            nc.sync.dma_start(out_words[:, h * P : (h + 1) * P], codes[:].bitcast(I32))

        halves = range(HALVES)
        sums = [products(h) for h in halves]
        s_banks = [scores(h, *sums[h]) for h in halves]
        spread_factors()
        exps = [exponentials(h, s_banks[h]) for h in halves]
        v_mx = [values(0)]
        looks = [shares(h, *exps[h]) for h in halves]
        w_mx = [weights(0, *looks[0])]
        v_mx.append(values(1))
        w_mx.append(weights(1, *looks[1]))
        v_mx.append(values(2))
        v_mx.append(values(3))
        for h in range(HALVES):
            result(h, w_mx[h], v_mx)
        for quad in range(4):
            queue = nc.scalar if quad % 2 else nc.sync
            queue.dma_start(
                out_2[0, 4 * quad : 4 * quad + 4, :].bitcast(I32),
                y_scales[32 * quad : 32 * quad + 4, :].bitcast(I32),
            )
